import numpy as np
import ml_dtypes


def mxq(x, axis, fmt="e4m3"):
    dtype, down = {"e4m3": (ml_dtypes.float8_e4m3fn, 7), "e5m2": (ml_dtypes.float8_e5m2, 14)}[fmt]
    v = np.moveaxis(np.asarray(x, np.float32).astype(ml_dtypes.bfloat16).astype(np.float64), axis, -1)
    blocks = v.reshape(v.shape[:-1] + (-1, 32))
    amax = np.abs(blocks).max(-1, keepdims=True)
    byte = np.maximum(np.where(amax > 0, np.frexp(amax)[1] - 1 + 127, 0) - down, 1)
    scale = np.exp2(byte - 127.0)
    codes = (blocks / scale).astype(np.float32).astype(dtype).astype(np.float64)
    return np.moveaxis((codes * scale).reshape(v.shape), -1, axis)


WIDE = False


def mx_kscale(k):
    if not WIDE:
        return np.ones(k)
    levels = np.array([10, -10, 5, -5, 0])
    if k % 512:
        return np.exp2(np.random.permutation(np.resize(levels, k // 32))).repeat(32)
    a = np.empty((k // 512, 16))
    for p in range(k // 512):
        a[p, :8] = np.random.permutation(np.resize(levels, 8))
        for g in range(8):
            far = levels[np.abs(levels - a[p, g]) >= 10]
            a[p, g + 8] = far[np.random.randint(len(far))]
    return np.exp2(a.ravel()).repeat(32)


def f64(x):
    return np.asarray(x).astype(np.float64)


def striped(idx):
    return np.tile(idx.reshape(-1, 16).T, (8, 1)).astype(np.uint16)


def unstriped(offs):
    return offs[:16].T.reshape(-1).astype(np.int64)


def d_silu(v):
    s = 1.0 / (1.0 + np.exp(-np.maximum(v, -700.0)))
    return s * (1.0 + v * (1.0 - s))


K, T, E, C, H, N = 384, 512, 6, 256, 512, 512
TOP = 3


def by_expert(wq, xq):
    return np.concatenate([wq[e].T @ xq[:, e * C:(e + 1) * C] for e in range(E)], axis=1)


def setup_inputs():
    n = np.random.standard_normal
    s = mx_kscale(N)[:, None]
    u = mx_kscale(H)
    deal = np.repeat(np.arange(E), C).reshape(TOP, T)[:, np.random.permutation(T)]
    deal = np.take_along_axis(deal, np.argsort(np.random.rand(TOP, T), axis=0), axis=0)
    for _ in range(8):
        s_, t_ = np.random.permutation(T).reshape(2, -1); r = np.random.randint(TOP, size=T // 2); x, y = deal[r, s_].copy(), deal[r, t_].copy()
        ok = ~((deal[:, s_] == y).any(0) | (deal[:, t_] == x).any(0)); deal[r[ok], s_[ok]] = y[ok]; deal[r[ok], t_[ok]] = x[ok]
    order = np.lexsort((np.random.rand(TOP * T), deal.reshape(-1)))
    slot_token = order % T; pos = np.empty(TOP * T, np.int64); pos[order] = np.arange(TOP * T); pos = pos.reshape(TOP, T)
    g = np.random.uniform(0.5, 1.5, (TOP, T)); g = g / g.sum(0)
    w_slot = np.empty(E * C)
    for r in range(TOP): w_slot[pos[r]] = g[r]
    return {
        "dyT": (n((N, T)) * s).astype(np.float32),
        "a": n((H, E * C)).astype(np.float32),
        "w2": (n((E, N, H)) / np.sqrt(N) / s[None] * u[None, None, :]).astype(np.float32),
        "w1": (n((E, H, K)) / np.sqrt(H) / u[None, :, None]).astype(np.float32),
        "gate": np.tile(w_slot, (N, 1)).astype(np.float32),
        "offs": striped(slot_token),
        "pos1": striped(pos[0]),
        "pos2": striped(pos[1]),
        "pos3": striped(pos[2]),
    }


def reference(dyT, a, w2, w1, gate, offs, pos1, pos2, pos3):
    idx = unstriped(offs)
    gq = mxq(f64(gate) * f64(dyT)[:, idx], 0, "e4m3")
    dh = by_expert(mxq(f64(w2), 1, "e4m3"), gq)
    da = dh * d_silu(f64(a))
    dx = by_expert(mxq(f64(w1), 1, "e4m3"), mxq(da, 0, "e4m3"))
    return dx[:, unstriped(pos1)] + dx[:, unstriped(pos2)] + dx[:, unstriped(pos3)]

@@ -1,0 +1,204 @@
+from contextlib import ExitStack
+
+import concourse.mybir as mybir
+
+K, T, E, C, H, N = 384, 512, 6, 256, 512, 512
+S = E * C
+FLOPS = 2 * S * (N * H + H * K)
+BYTES = 4 * (N * T + H * S + E * N * H + E * H * K + S + K * T) + 2 * 128 * (S + 3 * T) // 16
+
+F32 = mybir.dt.float32
+BF16 = mybir.dt.bfloat16
+U32 = mybir.dt.uint32
+U16 = mybir.dt.uint16
+U8 = mybir.dt.uint8
+FP8X4 = mybir.dt.float8_e4m3fn_x4
+ALU = mybir.AluOpType
+ACT = mybir.ActivationFunctionType
+
+P = 128
+PACK = 4
+KB = K // P
+HALF = 128
+LEAD = 4
+GATE_FIRST = 3 * C
+VECTOR_W1 = 10
+VECTOR_W2 = 3
+
+
+def tile_moe_bdx_mlp_silu_kernel(tc, dyT, a, w2, w1, gate, offs, pos1, pos2, pos3, out):
+    nc = tc.nc
+    with ExitStack() as ctx:
+        held = ctx.enter_context(tc.tile_pool(name="held", bufs=1))
+        ring = ctx.enter_context(tc.tile_pool(name="ring", bufs=1))
+        psum = ctx.enter_context(tc.psum_pool(name="psum", bufs=4))
+
+        offs_sb = held.tile([P, S // 16], U16, name="offs_sb")
+        pos_sb = [held.tile([P, T // 16], U16, name="pos_sb%d" % r) for r in range(3)]
+        dy_rows = dyT.rearrange("(p j) t -> p j t", j=PACK)
+        dy_sb = [held.tile([P, T], F32, name="dy_sb%d" % j) for j in range(PACK)]
+        gate_a = held.tile([P, GATE_FIRST], F32, name="gate_a")
+        gate_b = held.tile([P, S - GATE_FIRST], F32, name="gate_b")
+        a_rows = a.rearrange("(p t) s -> p t s", t=PACK)
+        a_sb = {}
+        w2_sb = {}
+        w1_sb = {}
+
+        def load_a(e):
+            a_sb[e] = ring.tile([P, PACK, C], F32, name="a_sb", bufs=4)
+            nc.sync.dma_start(out=a_sb[e][:], in_=a_rows[:, :, e * C:(e + 1) * C])
+
+        def load_w2(e):
+            w2_sb[e] = ring.tile([P, PACK, H], F32, name="w2_sb", tag="big", bufs=E)
+            nc.sync.dma_start(out=w2_sb[e][:], in_=w2[e].rearrange("(p j) i -> p j i", j=PACK))
+
+        def load_w1(e):
+            w1_sb[e] = held.tile([P, PACK, K], F32, name="w1_sb%d" % e)
+            nc.sync.dma_start(out=w1_sb[e][:], in_=w1[e].rearrange("(p j) k -> p j k", j=PACK))
+
+        nc.sync.dma_start(offs_sb[:], offs)
+        def load_dy(j):
+            nc.sync.dma_start(out=dy_sb[j][:], in_=dy_rows[:, j, :])
+
+        load_dy(0)
+        nc.sync.dma_start(out=gate_a[:], in_=gate[0:P, 0:GATE_FIRST])
+        load_a(0)
+        load_dy(1)
+        nc.sync.dma_start(out=gate_b[:], in_=gate[0:P, GATE_FIRST:S])
+        load_a(1)
+        load_dy(2)
+        load_w2(0)
+        load_dy(3)
+        load_w2(1)
+        for e in range(2, 4):
+            load_a(e)
+            load_w2(e)
+
+        def gate_of(e):
+            if (e + 1) * C <= GATE_FIRST:
+                return gate_a[:, e * C:(e + 1) * C]
+            return gate_b[:, e * C - GATE_FIRST:(e + 1) * C - GATE_FIRST]
+
+        g32 = {}
+
+        def gather_g(e):
+            g32[e] = ring.tile([P, PACK, C], F32, name="g32", bufs=LEAD)
+            cols = offs_sb[:, e * C // 16:(e + 1) * C // 16]
+            for j in range(PACK):
+                nc.vector.tensor_tensor(g32[e][:, j, :], dy_sb[j][:].indirect(cols), gate_of(e), ALU.mult)
+
+        def weave_out(ap):
+            return ap.rearrange("p (c i j) -> p c j i", i=2, j=PACK)
+
+        def weave_in(ap):
+            return ap.rearrange("p j (c i) -> p c j i", i=2)
+
+        def quantize(src, width, name, bufs, pool):
+            codes = pool.tile([P, width], U32, name=name + "_codes", bufs=bufs, align_bytes=64)
+            scales = pool.tile([P, width], U8, name=name + "_scales", bufs=bufs, align_bytes=64)
+            nc.vector.quantize_mx(out=codes[:].bitcast(FP8X4), scales=scales[:], in_=src)
+            return codes, scales
+
+        def mm(dst, lhs, lcols, rhs, rcols):
+            nc.tensor.matmul_mx(
+                out=dst,
+                lhsT=lhs[0][:, lcols].bitcast(FP8X4),
+                lhsT_scale=lhs[1][:, lcols],
+                rhs=rhs[0][:, rcols].bitcast(FP8X4),
+                rhs_scale=rhs[1][:, rcols],
+                start=True,
+                stop=True,
+            )
+
+        da_q = {}
+
+        def expert(e):
+            u = ring.tile([P, PACK * C], F32, name="u", bufs=3)
+            th = ring.tile([P, PACK * C], F32, name="th", bufs=3)
+            g16 = ring.tile([P, PACK * C], BF16, name="g16", bufs=2, align_bytes=64)
+            nc.scalar.copy(weave_out(g16[:]), weave_in(g32[e][:]))
+            w16 = ring.tile([P, PACK * H], BF16, name="w16", bufs=3, align_bytes=64)
+            cast = nc.vector.tensor_copy if e == VECTOR_W2 else nc.scalar.copy
+            cast(
+                w16[:].rearrange("p (t m j) -> p m j t", t=PACK, j=PACK),
+                w2_sb[e][:].rearrange("p j (m t) -> p m j t", t=PACK),
+            )
+            nc.scalar.activation(weave_out(u[:]), weave_in(a_sb[e][:]), ACT.Silu, scale=-1.0)
+            nc.scalar.activation(weave_out(th[:]), weave_in(a_sb[e][:]), ACT.Tanh, scale=0.5)
+            if e + 4 < E:
+                load_a(e + 4)
+                load_w2(e + 4)
+            g_q = quantize(g16[:], C, "g", 2, ring)
+            w_q = quantize(w16[:], H, "w2", 3, ring)
+            da16 = ring.tile([P, PACK * C], BF16, name="da16", bufs=2, align_bytes=64)
+            t1 = {}
+            for h in range(C // HALF):
+                dh = psum.tile([P, PACK, HALF], F32, name="dh")
+                for t in range(PACK):
+                    mm(dh[:, t, :], w_q, slice(t * P, (t + 1) * P), g_q, slice(h * HALF, (h + 1) * HALF))
+                cols = slice(h * PACK * HALF, (h + 1) * PACK * HALF)
+                t1[h] = ring.tile([P, PACK * HALF], F32, name="t1", bufs=4)
+                nc.vector.scalar_tensor_tensor(
+                    t1[h][:].rearrange("p (s t) -> p s t", t=PACK),
+                    u[:, cols].rearrange("p (s t) -> p s t", t=PACK),
+                    1.0,
+                    dh[:].rearrange("p t s -> p s t"),
+                    ALU.subtract,
+                    ALU.mult,
+                )
+            for h in range(C // HALF):
+                cols = slice(h * PACK * HALF, (h + 1) * PACK * HALF)
+                nc.vector.scalar_tensor_tensor(da16[:, cols], th[:, cols], 1.0, t1[h][:], ALU.add, ALU.mult)
+            da_q[e] = quantize(da16[:], C, "da", E, ring)
+
+        for e in range(LEAD):
+            gather_g(e)
+        for e in range(E):
+            expert(e)
+            if e == 1:
+                for r, pos in enumerate((pos1, pos2, pos3)):
+                    nc.sync.dma_start(pos_sb[r][:], pos)
+                for x in range(E):
+                    load_w1(x)
+            if e + LEAD < E:
+                gather_g(e + LEAD)
+
+        dxs = {}
+        for kb in range(KB):
+            dx = ring.tile([P, S], F32, name="dx", tag="big", bufs=E)
+            dxs[kb] = dx
+            for pair in range(E // 2):
+                if kb > 0 and pair == E // 2 - 1:
+                    v16 = ring.tile([P, 2 * PACK * P], BF16, name="v16_last", tag="hold%d" % kb, bufs=1, align_bytes=64)
+                else:
+                    v16 = ring.tile([P, 2 * PACK * P], BF16, name="v16", bufs=4, align_bytes=64)
+                for x in range(2):
+                    e = 2 * pair + x
+                    dst = weave_out(v16[:, x * PACK * P:(x + 1) * PACK * P])
+                    src = weave_in(w1_sb[e][:, :, kb * P:(kb + 1) * P])
+                    if kb * E + e < VECTOR_W1:
+                        nc.vector.tensor_copy(dst, src)
+                    else:
+                        nc.scalar.copy(dst, src)
+                v_q = quantize(v16[:], 2 * P, "w1", KB * E // 2, ring)
+                bank = psum.tile([P, 2 * C], F32, name="bank")
+                for x in range(2):
+                    mm(bank[:, x * C:(x + 1) * C], v_q, slice(x * P, (x + 1) * P), da_q[2 * pair + x], slice(0, C))
+                nc.scalar.activation(dx[:, pair * 2 * C:(pair + 1) * 2 * C], bank[:], ACT.Copy, scale=-0.5)
+        for kb in range(KB):
+            dx = dxs[kb]
+            acc = {}
+            for r in range(3):
+                for h in range(2):
+                    cols = pos_sb[r][:, h * 16:(h + 1) * 16]
+                    if kb + 1 < KB and (r, h) == (2, 0):
+                        nxt = ring.tile([P, T // 2], F32, name="acc_held", tag="hold%d" % (kb + 1), bufs=1, align_bytes=64)
+                    else:
+                        nxt = ring.tile([P, T // 2], F32, name="acc", bufs=10)
+                    if r == 0:
+                        nc.vector.tensor_copy(nxt[:], dx[:].indirect(cols))
+                    else:
+                        nc.vector.tensor_tensor(nxt[:], dx[:].indirect(cols), acc[h][:], ALU.add)
+                    acc[h] = nxt
+            for h in range(2):
+                nc.sync.dma_start(out=out[kb * P:(kb + 1) * P, h * (T // 2):(h + 1) * (T // 2)], in_=acc[h][:])

@@ -21,9 +21,9 @@ PACK = 4
 KB = K // P
 HALF = 128
 LEAD = 4
-GATE_FIRST = 3 * C
-VECTOR_W1 = 10
-VECTOR_W2 = 3
+GATE_FIRST = 2 * C
+VECTOR_W2 = (2, 4)
+PAIRS = E // 2
 
 
 def tile_moe_bdx_mlp_silu_kernel(tc, dyT, a, w2, w1, gate, offs, pos1, pos2, pos3, out):
@@ -31,7 +31,7 @@ def tile_moe_bdx_mlp_silu_kernel(tc, dyT, a, w2, w1, gate, offs, pos1, pos2, pos
     with ExitStack() as ctx:
         held = ctx.enter_context(tc.tile_pool(name="held", bufs=1))
         ring = ctx.enter_context(tc.tile_pool(name="ring", bufs=1))
-        psum = ctx.enter_context(tc.psum_pool(name="psum", bufs=4))
+        psum = ctx.enter_context(tc.psum_pool(name="psum", bufs=1))
 
         offs_sb = held.tile([P, S // 16], U16, name="offs_sb")
         pos_sb = [held.tile([P, T // 16], U16, name="pos_sb%d" % r) for r in range(3)]
@@ -40,26 +40,28 @@ def tile_moe_bdx_mlp_silu_kernel(tc, dyT, a, w2, w1, gate, offs, pos1, pos2, pos
         gate_a = held.tile([P, GATE_FIRST], F32, name="gate_a")
         gate_b = held.tile([P, S - GATE_FIRST], F32, name="gate_b")
         a_rows = a.rearrange("(p t) s -> p t s", t=PACK)
+        dh_banks = [psum.tile([P, PACK * HALF], F32, name="dh_bank%d" % b) for b in range(4)]
+        dx_banks = [dh_banks[2], dh_banks[3], psum.tile([P, 2 * C], F32, name="dx_bank")]
         a_sb = {}
         w2_sb = {}
         w1_sb = {}
+
+        def load_dy(j):
+            nc.sync.dma_start(out=dy_sb[j][:], in_=dy_rows[:, j, :])
 
         def load_a(e):
             a_sb[e] = ring.tile([P, PACK, C], F32, name="a_sb", bufs=4)
             nc.sync.dma_start(out=a_sb[e][:], in_=a_rows[:, :, e * C:(e + 1) * C])
 
         def load_w2(e):
-            w2_sb[e] = ring.tile([P, PACK, H], F32, name="w2_sb", tag="big", bufs=E)
-            nc.sync.dma_start(out=w2_sb[e][:], in_=w2[e].rearrange("(p j) i -> p j i", j=PACK))
+            w2_sb[e] = ring.tile([P, PACK * H], F32, name="w2_sb", tag="big", bufs=E, align_bytes=64)
+            nc.sync.dma_start(out=w2_sb[e][:], in_=w2[e].rearrange("(p j) i -> p (j i)", j=PACK))
 
         def load_w1(e):
             w1_sb[e] = held.tile([P, PACK, K], F32, name="w1_sb%d" % e)
             nc.sync.dma_start(out=w1_sb[e][:], in_=w1[e].rearrange("(p j) k -> p j k", j=PACK))
 
         nc.sync.dma_start(offs_sb[:], offs)
-        def load_dy(j):
-            nc.sync.dma_start(out=dy_sb[j][:], in_=dy_rows[:, j, :])
-
         load_dy(0)
         nc.sync.dma_start(out=gate_a[:], in_=gate[0:P, 0:GATE_FIRST])
         load_a(0)
@@ -70,9 +72,25 @@ def tile_moe_bdx_mlp_silu_kernel(tc, dyT, a, w2, w1, gate, offs, pos1, pos2, pos
         load_w2(0)
         load_dy(3)
         load_w2(1)
-        for e in range(2, 4):
-            load_a(e)
-            load_w2(e)
+        load_w2(2)
+        load_a(2)
+        load_w2(3)
+        load_a(3)
+        load_w1(0)
+        load_w2(4)
+
+        def later_loads(e):
+            if e == 0:
+                load_a(4)
+                load_w1(1)
+                load_w1(2)
+                load_w2(5)
+            if e == 1:
+                load_a(5)
+                for r, pos in enumerate((pos1, pos2, pos3)):
+                    nc.sync.dma_start(pos_sb[r][:], pos)
+                for x in range(3, E):
+                    load_w1(x)
 
         def gate_of(e):
             if (e + 1) * C <= GATE_FIRST:
@@ -93,9 +111,9 @@ def tile_moe_bdx_mlp_silu_kernel(tc, dyT, a, w2, w1, gate, offs, pos1, pos2, pos
         def weave_in(ap):
             return ap.rearrange("p j (c i) -> p c j i", i=2)
 
-        def quantize(src, width, name, bufs, pool):
-            codes = pool.tile([P, width], U32, name=name + "_codes", bufs=bufs, align_bytes=64)
-            scales = pool.tile([P, width], U8, name=name + "_scales", bufs=bufs, align_bytes=64)
+        def quantize(src, width, name, bufs):
+            codes = ring.tile([P, width], U32, name=name + "_codes", bufs=bufs, align_bytes=64)
+            scales = ring.tile([P, width], U8, name=name + "_scales", bufs=bufs, align_bytes=64)
             nc.vector.quantize_mx(out=codes[:].bitcast(FP8X4), scales=scales[:], in_=src)
             return codes, scales
 
@@ -110,95 +128,97 @@ def tile_moe_bdx_mlp_silu_kernel(tc, dyT, a, w2, w1, gate, offs, pos1, pos2, pos
                 stop=True,
             )
 
+        u = {}
+        th = {}
+        w16 = {}
         da_q = {}
 
-        def expert(e):
-            u = ring.tile([P, PACK * C], F32, name="u", bufs=3)
-            th = ring.tile([P, PACK * C], F32, name="th", bufs=3)
-            g16 = ring.tile([P, PACK * C], BF16, name="g16", bufs=2, align_bytes=64)
+        def front(e):
+            g16 = ring.tile([P, PACK * C], BF16, name="g16", bufs=4, align_bytes=64)
             nc.scalar.copy(weave_out(g16[:]), weave_in(g32[e][:]))
-            w16 = ring.tile([P, PACK * H], BF16, name="w16", bufs=3, align_bytes=64)
-            cast = nc.vector.tensor_copy if e == VECTOR_W2 else nc.scalar.copy
+            w16[e] = ring.tile([P, PACK * H], BF16, name="w16", bufs=3, align_bytes=64)
+            cast = nc.vector.tensor_copy if e in VECTOR_W2 else nc.scalar.copy
             cast(
-                w16[:].rearrange("p (t m j) -> p m j t", t=PACK, j=PACK),
-                w2_sb[e][:].rearrange("p j (m t) -> p m j t", t=PACK),
+                w16[e][:].rearrange("p (t m j) -> p m j t", t=PACK, j=PACK),
+                w2_sb[e][:].rearrange("p (j m t) -> p m j t", t=PACK, j=PACK),
             )
-            nc.scalar.activation(weave_out(u[:]), weave_in(a_sb[e][:]), ACT.Silu, scale=-1.0)
-            nc.scalar.activation(weave_out(th[:]), weave_in(a_sb[e][:]), ACT.Tanh, scale=0.5)
-            if e + 4 < E:
-                load_a(e + 4)
-                load_w2(e + 4)
-            g_q = quantize(g16[:], C, "g", 2, ring)
-            w_q = quantize(w16[:], H, "w2", 3, ring)
-            da16 = ring.tile([P, PACK * C], BF16, name="da16", bufs=2, align_bytes=64)
-            t1 = {}
+            u[e] = ring.tile([P, PACK * C], F32, name="u", bufs=3)
+            th[e] = ring.tile([P, PACK * C], F32, name="th", bufs=3)
+            nc.scalar.activation(weave_out(u[e][:]), weave_in(a_sb[e][:]), ACT.Silu, scale=-1.0)
+            nc.scalar.activation(weave_out(th[e][:]), weave_in(a_sb[e][:]), ACT.Tanh, scale=0.5)
+            later_loads(e)
+            g_q = quantize(g16[:], C, "g", 2)
+            w_q = quantize(w16[e][:], H, "w2", 3)
             for h in range(C // HALF):
-                dh = psum.tile([P, PACK, HALF], F32, name="dh")
+                dh = dh_banks[(2 * e + h) % 4]
                 for t in range(PACK):
-                    mm(dh[:, t, :], w_q, slice(t * P, (t + 1) * P), g_q, slice(h * HALF, (h + 1) * HALF))
+                    mm(dh[:, t * HALF:(t + 1) * HALF], w_q, slice(t * P, (t + 1) * P), g_q, slice(h * HALF, (h + 1) * HALF))
+
+        def back(e):
+            if e + 1 < E:
+                t1 = w16[e + 1][:].bitcast(F32)
+            else:
+                t1_last = held.tile([P, PACK * C], F32, name="t1_last")
+                t1 = t1_last[:]
+            da16 = ring.tile([P, PACK * C], BF16, name="da16", bufs=3, align_bytes=64)
+            for h in range(C // HALF):
                 cols = slice(h * PACK * HALF, (h + 1) * PACK * HALF)
-                t1[h] = ring.tile([P, PACK * HALF], F32, name="t1", bufs=4)
                 nc.vector.scalar_tensor_tensor(
-                    t1[h][:].rearrange("p (s t) -> p s t", t=PACK),
-                    u[:, cols].rearrange("p (s t) -> p s t", t=PACK),
+                    t1[:, cols].rearrange("p (s t) -> p s t", t=PACK),
+                    u[e][:, cols].rearrange("p (s t) -> p s t", t=PACK),
                     1.0,
-                    dh[:].rearrange("p t s -> p s t"),
+                    dh_banks[(2 * e + h) % 4][:].rearrange("p (t s) -> p s t", t=PACK),
                     ALU.subtract,
                     ALU.mult,
                 )
             for h in range(C // HALF):
                 cols = slice(h * PACK * HALF, (h + 1) * PACK * HALF)
-                nc.vector.scalar_tensor_tensor(da16[:, cols], th[:, cols], 1.0, t1[h][:], ALU.add, ALU.mult)
-            da_q[e] = quantize(da16[:], C, "da", E, ring)
+                nc.vector.scalar_tensor_tensor(da16[:, cols], th[e][:, cols], 1.0, t1[:, cols], ALU.add, ALU.mult)
+            da_q[e] = quantize(da16[:], C, "da", E)
 
         for e in range(LEAD):
             gather_g(e)
         for e in range(E):
-            expert(e)
-            if e == 1:
-                for r, pos in enumerate((pos1, pos2, pos3)):
-                    nc.sync.dma_start(pos_sb[r][:], pos)
-                for x in range(E):
-                    load_w1(x)
+            front(e)
+            if e > 0:
+                back(e - 1)
             if e + LEAD < E:
                 gather_g(e + LEAD)
+        back(E - 1)
 
         dxs = {}
         for kb in range(KB):
-            dx = ring.tile([P, S], F32, name="dx", tag="big", bufs=E)
-            dxs[kb] = dx
-            for pair in range(E // 2):
-                if kb > 0 and pair == E // 2 - 1:
-                    v16 = ring.tile([P, 2 * PACK * P], BF16, name="v16_last", tag="hold%d" % kb, bufs=1, align_bytes=64)
+            v_q = {}
+            for pair in range(PAIRS):
+                if kb == KB - 1:
+                    v16 = w2_sb[E - 1][:].bitcast(BF16)[:, pair * 2 * PACK * P:(pair + 1) * 2 * PACK * P]
                 else:
-                    v16 = ring.tile([P, 2 * PACK * P], BF16, name="v16", bufs=4, align_bytes=64)
+                    v16_tile = ring.tile([P, 2 * PACK * P], BF16, name="v16_tile", bufs=2 * PAIRS, align_bytes=64)
+                    v16 = v16_tile[:]
                 for x in range(2):
-                    e = 2 * pair + x
-                    dst = weave_out(v16[:, x * PACK * P:(x + 1) * PACK * P])
-                    src = weave_in(w1_sb[e][:, :, kb * P:(kb + 1) * P])
-                    if kb * E + e < VECTOR_W1:
-                        nc.vector.tensor_copy(dst, src)
-                    else:
-                        nc.scalar.copy(dst, src)
-                v_q = quantize(v16[:], 2 * P, "w1", KB * E // 2, ring)
-                bank = psum.tile([P, 2 * C], F32, name="bank")
+                    cast = nc.vector.tensor_copy if kb == 0 else nc.scalar.copy
+                    cast(weave_out(v16[:, x * PACK * P:(x + 1) * PACK * P]), weave_in(w1_sb[2 * pair + x][:, :, kb * P:(kb + 1) * P]))
+                v_q[pair] = quantize(v16, 2 * P, "w1", KB * PAIRS)
+            dxs[kb] = ring.tile([P, S], F32, name="dx", tag="big", bufs=E, align_bytes=64)
+            for pair in range(PAIRS):
+                bank = dx_banks[pair]
                 for x in range(2):
-                    mm(bank[:, x * C:(x + 1) * C], v_q, slice(x * P, (x + 1) * P), da_q[2 * pair + x], slice(0, C))
-                nc.scalar.activation(dx[:, pair * 2 * C:(pair + 1) * 2 * C], bank[:], ACT.Copy, scale=-0.5)
+                    mm(bank[:, x * C:(x + 1) * C], v_q[pair], slice(x * P, (x + 1) * P), da_q[2 * pair + x], slice(0, C))
+                nc.scalar.activation(dxs[kb][:, pair * 2 * C:(pair + 1) * 2 * C], bank[:], ACT.Copy, scale=-0.5)
         for kb in range(KB):
-            dx = dxs[kb]
             acc = {}
             for r in range(3):
                 for h in range(2):
                     cols = pos_sb[r][:, h * 16:(h + 1) * 16]
-                    if kb + 1 < KB and (r, h) == (2, 0):
-                        nxt = ring.tile([P, T // 2], F32, name="acc_held", tag="hold%d" % (kb + 1), bufs=1, align_bytes=64)
+                    if (kb, r, h) == (KB - 2, 1, 0):
+                        nxt = w2_sb[E - 1][:, (PAIRS - 1) * PACK * P:(PAIRS - 1) * PACK * P + T // 2]
                     else:
-                        nxt = ring.tile([P, T // 2], F32, name="acc", bufs=10)
+                        acc_tile = ring.tile([P, T // 2], F32, name="acc_tile", bufs=8)
+                        nxt = acc_tile[:]
                     if r == 0:
-                        nc.vector.tensor_copy(nxt[:], dx[:].indirect(cols))
+                        nc.vector.tensor_copy(nxt, dxs[kb][:].indirect(cols))
                     else:
-                        nc.vector.tensor_tensor(nxt[:], dx[:].indirect(cols), acc[h][:], ALU.add)
+                        nc.vector.tensor_tensor(nxt, dxs[kb][:].indirect(cols), acc[h], ALU.add)
                     acc[h] = nxt
             for h in range(2):
-                nc.sync.dma_start(out=out[kb * P:(kb + 1) * P, h * (T // 2):(h + 1) * (T // 2)], in_=acc[h][:])
+                nc.sync.dma_start(out=out[kb * P:(kb + 1) * P, h * (T // 2):(h + 1) * (T // 2)], in_=acc[h])

@@ -21,7 +21,7 @@ PACK = 4
 KB = K // P
 HALF = 128
 LEAD = 4
-GATE_FIRST = 2 * C
+GATE_CUTS = (0, 1, 3, E)
 VECTOR_W2 = (2, 4)
 PAIRS = E // 2
 
@@ -37,8 +37,7 @@ def tile_moe_bdx_mlp_silu_kernel(tc, dyT, a, w2, w1, gate, offs, pos1, pos2, pos
         pos_sb = [held.tile([P, T // 16], U16, name="pos_sb%d" % r) for r in range(3)]
         dy_rows = dyT.rearrange("(p j) t -> p j t", j=PACK)
         dy_sb = [held.tile([P, T], F32, name="dy_sb%d" % j) for j in range(PACK)]
-        gate_a = held.tile([P, GATE_FIRST], F32, name="gate_a")
-        gate_b = held.tile([P, S - GATE_FIRST], F32, name="gate_b")
+        gate_sb = {}
         a_rows = a.rearrange("(p t) s -> p t s", t=PACK)
         dh_banks = [psum.tile([P, PACK * HALF], F32, name="dh_bank%d" % b) for b in range(4)]
         dx_banks = [dh_banks[2], dh_banks[3], psum.tile([P, 2 * C], F32, name="dx_bank")]
@@ -48,6 +47,13 @@ def tile_moe_bdx_mlp_silu_kernel(tc, dyT, a, w2, w1, gate, offs, pos1, pos2, pos
 
         def load_dy(j):
             nc.sync.dma_start(out=dy_sb[j][:], in_=dy_rows[:, j, :])
+
+        def load_gate(piece):
+            first, last = GATE_CUTS[piece], GATE_CUTS[piece + 1]
+            tile = held.tile([P, (last - first) * C], F32, name="gate_sb%d" % piece)
+            nc.sync.dma_start(out=tile[:], in_=gate[0:P, first * C:last * C])
+            for e in range(first, last):
+                gate_sb[e] = tile[:, (e - first) * C:(e - first + 1) * C]
 
         def load_a(e):
             a_sb[e] = ring.tile([P, PACK, C], F32, name="a_sb", bufs=4)
@@ -63,14 +69,15 @@ def tile_moe_bdx_mlp_silu_kernel(tc, dyT, a, w2, w1, gate, offs, pos1, pos2, pos
 
         nc.sync.dma_start(offs_sb[:], offs)
         load_dy(0)
-        nc.sync.dma_start(out=gate_a[:], in_=gate[0:P, 0:GATE_FIRST])
-        load_a(0)
+        load_gate(0)
+        load_gate(1)
         load_dy(1)
-        nc.sync.dma_start(out=gate_b[:], in_=gate[0:P, GATE_FIRST:S])
-        load_a(1)
+        load_a(0)
         load_dy(2)
         load_w2(0)
         load_dy(3)
+        load_a(1)
+        load_gate(2)
         load_w2(1)
         load_w2(2)
         load_a(2)
@@ -92,18 +99,13 @@ def tile_moe_bdx_mlp_silu_kernel(tc, dyT, a, w2, w1, gate, offs, pos1, pos2, pos
                 for x in range(3, E):
                     load_w1(x)
 
-        def gate_of(e):
-            if (e + 1) * C <= GATE_FIRST:
-                return gate_a[:, e * C:(e + 1) * C]
-            return gate_b[:, e * C - GATE_FIRST:(e + 1) * C - GATE_FIRST]
-
         g32 = {}
 
         def gather_g(e):
             g32[e] = ring.tile([P, PACK, C], F32, name="g32", bufs=LEAD)
             cols = offs_sb[:, e * C // 16:(e + 1) * C // 16]
             for j in range(PACK):
-                nc.vector.tensor_tensor(g32[e][:, j, :], dy_sb[j][:].indirect(cols), gate_of(e), ALU.mult)
+                nc.vector.tensor_tensor(g32[e][:, j, :], dy_sb[j][:].indirect(cols), gate_sb[e], ALU.mult)
 
         def weave_out(ap):
             return ap.rearrange("p (c i j) -> p c j i", i=2, j=PACK)
@@ -186,9 +188,8 @@ def tile_moe_bdx_mlp_silu_kernel(tc, dyT, a, w2, w1, gate, offs, pos1, pos2, pos
                 gather_g(e + LEAD)
         back(E - 1)
 
-        dxs = {}
+        v_q = {}
         for kb in range(KB):
-            v_q = {}
             for pair in range(PAIRS):
                 if kb == KB - 1:
                     v16 = w2_sb[E - 1][:].bitcast(BF16)[:, pair * 2 * PACK * P:(pair + 1) * 2 * PACK * P]
@@ -198,23 +199,22 @@ def tile_moe_bdx_mlp_silu_kernel(tc, dyT, a, w2, w1, gate, offs, pos1, pos2, pos
                 for x in range(2):
                     cast = nc.vector.tensor_copy if kb == 0 else nc.scalar.copy
                     cast(weave_out(v16[:, x * PACK * P:(x + 1) * PACK * P]), weave_in(w1_sb[2 * pair + x][:, :, kb * P:(kb + 1) * P]))
-                v_q[pair] = quantize(v16, 2 * P, "w1", KB * PAIRS)
+                v_q[kb, pair] = quantize(v16, 2 * P, "w1", KB * PAIRS)
+        dxs = {}
+        for kb in range(KB):
             dxs[kb] = ring.tile([P, S], F32, name="dx", tag="big", bufs=E, align_bytes=64)
             for pair in range(PAIRS):
                 bank = dx_banks[pair]
                 for x in range(2):
-                    mm(bank[:, x * C:(x + 1) * C], v_q[pair], slice(x * P, (x + 1) * P), da_q[2 * pair + x], slice(0, C))
+                    mm(bank[:, x * C:(x + 1) * C], v_q[kb, pair], slice(x * P, (x + 1) * P), da_q[2 * pair + x], slice(0, C))
                 nc.scalar.activation(dxs[kb][:, pair * 2 * C:(pair + 1) * 2 * C], bank[:], ACT.Copy, scale=-0.5)
         for kb in range(KB):
             acc = {}
             for r in range(3):
                 for h in range(2):
                     cols = pos_sb[r][:, h * 16:(h + 1) * 16]
-                    if (kb, r, h) == (KB - 2, 1, 0):
-                        nxt = w2_sb[E - 1][:, (PAIRS - 1) * PACK * P:(PAIRS - 1) * PACK * P + T // 2]
-                    else:
-                        acc_tile = ring.tile([P, T // 2], F32, name="acc_tile", bufs=8)
-                        nxt = acc_tile[:]
+                    acc_tile = ring.tile([P, T // 2], F32, name="acc_tile", bufs=8)
+                    nxt = acc_tile[:]
                     if r == 0:
                         nc.vector.tensor_copy(nxt, dxs[kb][:].indirect(cols))
                     else:

@@ -197,7 +197,7 @@ def tile_moe_bdx_mlp_silu_kernel(tc, dyT, a, w2, w1, gate, offs, pos1, pos2, pos
                     v16_tile = ring.tile([P, 2 * PACK * P], BF16, name="v16_tile", bufs=2 * PAIRS, align_bytes=64)
                     v16 = v16_tile[:]
                 for x in range(2):
-                    cast = nc.vector.tensor_copy if kb == 0 else nc.scalar.copy
+                    cast = nc.vector.tensor_copy if (kb, pair) == (0, 0) else nc.scalar.copy
                     cast(weave_out(v16[:, x * PACK * P:(x + 1) * PACK * P]), weave_in(w1_sb[2 * pair + x][:, :, kb * P:(kb + 1) * P]))
                 v_q[kb, pair] = quantize(v16, 2 * P, "w1", KB * PAIRS)
         dxs = {}

@@ -18,12 +18,18 @@ ACT = mybir.ActivationFunctionType
 
 P = 128
 PACK = 4
-KB = K // P
-HALF = 128
-LEAD = 4
-GATE_CUTS = (0, 1, 3, E)
-VECTOR_W2 = (2, 4)
+PER_COLUMN = 16
+RUN = 2
+K_BLOCKS = K // P
+SLOT_HALF = C // 2
+TOKEN_HALF = T // 2
 PAIRS = E // 2
+DH_BANKS = 4
+G_AHEAD = 4
+A_BUFS = 4
+GATE_CUTS = (0, 1, 3, E)
+VECTOR_W2 = range(2, E, 2)
+VECTOR_W1_PAIRS = 2
 
 
 def tile_moe_bdx_mlp_silu_kernel(tc, dyT, a, w2, w1, gate, offs, pos1, pos2, pos3, out):
@@ -33,13 +39,13 @@ def tile_moe_bdx_mlp_silu_kernel(tc, dyT, a, w2, w1, gate, offs, pos1, pos2, pos
         ring = ctx.enter_context(tc.tile_pool(name="ring", bufs=1))
         psum = ctx.enter_context(tc.psum_pool(name="psum", bufs=1))
 
-        offs_sb = held.tile([P, S // 16], U16, name="offs_sb")
-        pos_sb = [held.tile([P, T // 16], U16, name="pos_sb%d" % r) for r in range(3)]
+        offs_sb = held.tile([P, S // PER_COLUMN], U16, name="offs_sb")
+        pos_sb = [held.tile([P, T // PER_COLUMN], U16, name="pos_sb%d" % r) for r in range(3)]
         dy_rows = dyT.rearrange("(p j) t -> p j t", j=PACK)
         dy_sb = [held.tile([P, T], F32, name="dy_sb%d" % j) for j in range(PACK)]
         gate_sb = {}
         a_rows = a.rearrange("(p t) s -> p t s", t=PACK)
-        dh_banks = [psum.tile([P, PACK * HALF], F32, name="dh_bank%d" % b) for b in range(4)]
+        dh_banks = [psum.tile([P, PACK * SLOT_HALF], F32, name="dh_bank%d" % b) for b in range(DH_BANKS)]
         dx_banks = [dh_banks[2], dh_banks[3], psum.tile([P, 2 * C], F32, name="dx_bank")]
         a_sb = {}
         w2_sb = {}
@@ -56,15 +62,15 @@ def tile_moe_bdx_mlp_silu_kernel(tc, dyT, a, w2, w1, gate, offs, pos1, pos2, pos
                 gate_sb[e] = tile[:, (e - first) * C:(e - first + 1) * C]
 
         def load_a(e):
-            a_sb[e] = ring.tile([P, PACK, C], F32, name="a_sb", bufs=4)
+            a_sb[e] = ring.tile([P, PACK, C], F32, name="a_sb", bufs=A_BUFS)
             nc.sync.dma_start(out=a_sb[e][:], in_=a_rows[:, :, e * C:(e + 1) * C])
 
         def load_w2(e):
-            w2_sb[e] = ring.tile([P, PACK * H], F32, name="w2_sb", tag="big", bufs=E, align_bytes=64)
+            w2_sb[e] = ring.tile([P, PACK * H], F32, name="w2_sb", tag="w2_or_dx", bufs=E, align_bytes=64)
             nc.sync.dma_start(out=w2_sb[e][:], in_=w2[e].rearrange("(p j) i -> p (j i)", j=PACK))
 
         def load_w1(e):
-            w1_sb[e] = held.tile([P, PACK, K], F32, name="w1_sb%d" % e)
+            w1_sb[e] = ring.tile([P, PACK, K], F32, name="w1_sb%d" % e, tag="w1_%d" % e, bufs=1)
             nc.sync.dma_start(out=w1_sb[e][:], in_=w1[e].rearrange("(p j) k -> p j k", j=PACK))
 
         nc.sync.dma_start(offs_sb[:], offs)
@@ -79,39 +85,35 @@ def tile_moe_bdx_mlp_silu_kernel(tc, dyT, a, w2, w1, gate, offs, pos1, pos2, pos
         load_a(1)
         load_gate(2)
         load_w2(1)
-        load_w2(2)
-        load_a(2)
-        load_w2(3)
-        load_a(3)
-        load_w1(0)
-        load_w2(4)
+        for e in range(2, A_BUFS):
+            load_w2(e)
+            load_a(e)
+        load_w2(A_BUFS)
 
         def later_loads(e):
-            if e == 0:
-                load_a(4)
-                load_w1(1)
-                load_w1(2)
-                load_w2(5)
-            if e == 1:
-                load_a(5)
+            if e + A_BUFS < E:
+                load_a(e + A_BUFS)
+            if e + A_BUFS + 1 < E:
+                load_w2(e + A_BUFS + 1)
+            if e + A_BUFS == E - 1:
                 for r, pos in enumerate((pos1, pos2, pos3)):
                     nc.sync.dma_start(pos_sb[r][:], pos)
-                for x in range(3, E):
+                for x in range(E):
                     load_w1(x)
 
         g32 = {}
 
         def gather_g(e):
-            g32[e] = ring.tile([P, PACK, C], F32, name="g32", bufs=LEAD)
-            cols = offs_sb[:, e * C // 16:(e + 1) * C // 16]
+            g32[e] = ring.tile([P, PACK, C], F32, name="g32", bufs=G_AHEAD)
+            entries = offs_sb[:, e * C // PER_COLUMN:(e + 1) * C // PER_COLUMN]
             for j in range(PACK):
-                nc.vector.tensor_tensor(g32[e][:, j, :], dy_sb[j][:].indirect(cols), gate_sb[e], ALU.mult)
+                nc.vector.tensor_tensor(g32[e][:, j, :], dy_sb[j][:].indirect(entries), gate_sb[e], ALU.mult)
 
         def weave_out(ap):
-            return ap.rearrange("p (c i j) -> p c j i", i=2, j=PACK)
+            return ap.rearrange("p (c i j) -> p c j i", i=RUN, j=PACK)
 
         def weave_in(ap):
-            return ap.rearrange("p j (c i) -> p c j i", i=2)
+            return ap.rearrange("p j (c i) -> p c j i", i=RUN)
 
         def quantize(src, width, name, bufs):
             codes = ring.tile([P, width], U32, name=name + "_codes", bufs=bufs, align_bytes=64)
@@ -119,29 +121,29 @@ def tile_moe_bdx_mlp_silu_kernel(tc, dyT, a, w2, w1, gate, offs, pos1, pos2, pos
             nc.vector.quantize_mx(out=codes[:].bitcast(FP8X4), scales=scales[:], in_=src)
             return codes, scales
 
-        def mm(dst, lhs, lcols, rhs, rcols):
+        def matmul(dst, lhs, lhs_cols, rhs, rhs_cols):
             nc.tensor.matmul_mx(
                 out=dst,
-                lhsT=lhs[0][:, lcols].bitcast(FP8X4),
-                lhsT_scale=lhs[1][:, lcols],
-                rhs=rhs[0][:, rcols].bitcast(FP8X4),
-                rhs_scale=rhs[1][:, rcols],
+                lhsT=lhs[0][:, lhs_cols].bitcast(FP8X4),
+                lhsT_scale=lhs[1][:, lhs_cols],
+                rhs=rhs[0][:, rhs_cols].bitcast(FP8X4),
+                rhs_scale=rhs[1][:, rhs_cols],
                 start=True,
                 stop=True,
             )
 
         u = {}
         th = {}
-        w16 = {}
+        w2_16 = {}
         da_q = {}
 
-        def front(e):
+        def make_dh(e):
             g16 = ring.tile([P, PACK * C], BF16, name="g16", bufs=4, align_bytes=64)
             nc.scalar.copy(weave_out(g16[:]), weave_in(g32[e][:]))
-            w16[e] = ring.tile([P, PACK * H], BF16, name="w16", bufs=3, align_bytes=64)
+            w2_16[e] = ring.tile([P, PACK * H], BF16, name="w2_16", bufs=3, align_bytes=64)
             cast = nc.vector.tensor_copy if e in VECTOR_W2 else nc.scalar.copy
             cast(
-                w16[e][:].rearrange("p (t m j) -> p m j t", t=PACK, j=PACK),
+                w2_16[e][:].rearrange("p (t m j) -> p m j t", t=PACK, j=PACK),
                 w2_sb[e][:].rearrange("p (j m t) -> p m j t", t=PACK, j=PACK),
             )
             u[e] = ring.tile([P, PACK * C], F32, name="u", bufs=3)
@@ -150,75 +152,91 @@ def tile_moe_bdx_mlp_silu_kernel(tc, dyT, a, w2, w1, gate, offs, pos1, pos2, pos
             nc.scalar.activation(weave_out(th[e][:]), weave_in(a_sb[e][:]), ACT.Tanh, scale=0.5)
             later_loads(e)
             g_q = quantize(g16[:], C, "g", 2)
-            w_q = quantize(w16[e][:], H, "w2", 3)
-            for h in range(C // HALF):
-                dh = dh_banks[(2 * e + h) % 4]
+            w2_q = quantize(w2_16[e][:], H, "w2", 3)
+            for h in range(2):
+                dh = dh_banks[(2 * e + h) % DH_BANKS]
                 for t in range(PACK):
-                    mm(dh[:, t * HALF:(t + 1) * HALF], w_q, slice(t * P, (t + 1) * P), g_q, slice(h * HALF, (h + 1) * HALF))
+                    matmul(
+                        dh[:, t * SLOT_HALF:(t + 1) * SLOT_HALF],
+                        w2_q, slice(t * P, (t + 1) * P),
+                        g_q, slice(h * SLOT_HALF, (h + 1) * SLOT_HALF),
+                    )
 
-        def back(e):
+        def make_da(e):
             if e + 1 < E:
-                t1 = w16[e + 1][:].bitcast(F32)
+                partial = w2_16[e + 1][:].bitcast(F32)
             else:
-                t1_last = held.tile([P, PACK * C], F32, name="t1_last")
-                t1 = t1_last[:]
+                partial_last = held.tile([P, PACK * C], F32, name="partial_last")
+                partial = partial_last[:]
             da16 = ring.tile([P, PACK * C], BF16, name="da16", bufs=3, align_bytes=64)
-            for h in range(C // HALF):
-                cols = slice(h * PACK * HALF, (h + 1) * PACK * HALF)
+            for h in range(2):
+                cols = slice(h * PACK * SLOT_HALF, (h + 1) * PACK * SLOT_HALF)
                 nc.vector.scalar_tensor_tensor(
-                    t1[:, cols].rearrange("p (s t) -> p s t", t=PACK),
+                    partial[:, cols].rearrange("p (s t) -> p s t", t=PACK),
                     u[e][:, cols].rearrange("p (s t) -> p s t", t=PACK),
                     1.0,
-                    dh_banks[(2 * e + h) % 4][:].rearrange("p (t s) -> p s t", t=PACK),
+                    dh_banks[(2 * e + h) % DH_BANKS][:].rearrange("p (t s) -> p s t", t=PACK),
                     ALU.subtract,
                     ALU.mult,
                 )
-            for h in range(C // HALF):
-                cols = slice(h * PACK * HALF, (h + 1) * PACK * HALF)
-                nc.vector.scalar_tensor_tensor(da16[:, cols], th[e][:, cols], 1.0, t1[:, cols], ALU.add, ALU.mult)
+            for h in range(2):
+                cols = slice(h * PACK * SLOT_HALF, (h + 1) * PACK * SLOT_HALF)
+                nc.vector.scalar_tensor_tensor(da16[:, cols], th[e][:, cols], 1.0, partial[:, cols], ALU.add, ALU.mult)
             da_q[e] = quantize(da16[:], C, "da", E)
 
-        for e in range(LEAD):
+        for e in range(G_AHEAD):
             gather_g(e)
         for e in range(E):
-            front(e)
+            make_dh(e)
             if e > 0:
-                back(e - 1)
-            if e + LEAD < E:
-                gather_g(e + LEAD)
-        back(E - 1)
+                make_da(e - 1)
+            if e + G_AHEAD < E:
+                gather_g(e + G_AHEAD)
+        make_da(E - 1)
 
-        v_q = {}
-        for kb in range(KB):
+        pair_width = 2 * PACK * P
+        w1_q = {}
+        for kb in range(K_BLOCKS):
             for pair in range(PAIRS):
-                if kb == KB - 1:
-                    v16 = w2_sb[E - 1][:].bitcast(BF16)[:, pair * 2 * PACK * P:(pair + 1) * 2 * PACK * P]
+                if kb == K_BLOCKS - 1:
+                    w1_16 = w2_sb[E - 1][:].bitcast(BF16)[:, pair * pair_width:(pair + 1) * pair_width]
                 else:
-                    v16_tile = ring.tile([P, 2 * PACK * P], BF16, name="v16_tile", bufs=2 * PAIRS, align_bytes=64)
-                    v16 = v16_tile[:]
+                    w1_16_tile = ring.tile([P, pair_width], BF16, name="w1_16_tile", bufs=2 * PAIRS, align_bytes=64)
+                    w1_16 = w1_16_tile[:]
                 for x in range(2):
-                    cast = nc.vector.tensor_copy if (kb, pair) == (0, 0) else nc.scalar.copy
-                    cast(weave_out(v16[:, x * PACK * P:(x + 1) * PACK * P]), weave_in(w1_sb[2 * pair + x][:, :, kb * P:(kb + 1) * P]))
-                v_q[kb, pair] = quantize(v16, 2 * P, "w1", KB * PAIRS)
-        dxs = {}
-        for kb in range(KB):
-            dxs[kb] = ring.tile([P, S], F32, name="dx", tag="big", bufs=E, align_bytes=64)
+                    cast = nc.vector.tensor_copy if kb == 0 and pair < VECTOR_W1_PAIRS else nc.scalar.copy
+                    cast(
+                        weave_out(w1_16[:, x * PACK * P:(x + 1) * PACK * P]),
+                        weave_in(w1_sb[2 * pair + x][:, :, kb * P:(kb + 1) * P]),
+                    )
+                w1_q[kb, pair] = quantize(w1_16, 2 * P, "w1", K_BLOCKS * PAIRS)
+
+        dx = {}
+        for kb in range(K_BLOCKS):
+            if kb == 0:
+                dx[kb] = ring.tile([P, S], F32, name="dx_first", tag="w1_%d" % (E - 1), bufs=1)
+            else:
+                dx[kb] = ring.tile([P, S], F32, name="dx", tag="w2_or_dx", bufs=E, align_bytes=64)
             for pair in range(PAIRS):
                 bank = dx_banks[pair]
                 for x in range(2):
-                    mm(bank[:, x * C:(x + 1) * C], v_q[kb, pair], slice(x * P, (x + 1) * P), da_q[2 * pair + x], slice(0, C))
-                nc.scalar.activation(dxs[kb][:, pair * 2 * C:(pair + 1) * 2 * C], bank[:], ACT.Copy, scale=-0.5)
-        for kb in range(KB):
-            acc = {}
+                    matmul(
+                        bank[:, x * C:(x + 1) * C],
+                        w1_q[kb, pair], slice(x * P, (x + 1) * P),
+                        da_q[2 * pair + x], slice(0, C),
+                    )
+                nc.scalar.activation(dx[kb][:, pair * 2 * C:(pair + 1) * 2 * C], bank[:], ACT.Copy, scale=-0.5)
+
+        for kb in range(K_BLOCKS):
+            total = {}
             for r in range(3):
                 for h in range(2):
-                    cols = pos_sb[r][:, h * 16:(h + 1) * 16]
-                    acc_tile = ring.tile([P, T // 2], F32, name="acc_tile", bufs=8)
-                    nxt = acc_tile[:]
+                    entries = pos_sb[r][:, h * TOKEN_HALF // PER_COLUMN:(h + 1) * TOKEN_HALF // PER_COLUMN]
+                    running = ring.tile([P, TOKEN_HALF], F32, name="running", bufs=8)
                     if r == 0:
-                        nc.vector.tensor_copy(nxt, dxs[kb][:].indirect(cols))
+                        nc.vector.tensor_copy(running[:], dx[kb][:].indirect(entries))
                     else:
-                        nc.vector.tensor_tensor(nxt, dxs[kb][:].indirect(cols), acc[h], ALU.add)
-                    acc[h] = nxt
+                        nc.vector.tensor_tensor(running[:], dx[kb][:].indirect(entries), total[h][:], ALU.add)
+                    total[h] = running
             for h in range(2):
-                nc.sync.dma_start(out=out[kb * P:(kb + 1) * P, h * (T // 2):(h + 1) * (T // 2)], in_=acc[h])
+                nc.sync.dma_start(out=out[kb * P:(kb + 1) * P, h * TOKEN_HALF:(h + 1) * TOKEN_HALF], in_=total[h][:])

from contextlib import ExitStack

import concourse.mybir as mybir

K, T, E, C, H, N = 384, 512, 6, 256, 512, 512
S = E * C
FLOPS = 2 * S * (N * H + H * K)
BYTES = 4 * (N * T + H * S + E * N * H + E * H * K + S + K * T) + 2 * 128 * (S + 3 * T) // 16

F32 = mybir.dt.float32
BF16 = mybir.dt.bfloat16
U32 = mybir.dt.uint32
U16 = mybir.dt.uint16
U8 = mybir.dt.uint8
FP8X4 = mybir.dt.float8_e4m3fn_x4
ALU = mybir.AluOpType
ACT = mybir.ActivationFunctionType

P = 128
PACK = 4
PER_COLUMN = 16
RUN = 2
K_BLOCKS = K // P
SLOT_HALF = C // 2
TOKEN_HALF = T // 2
PAIRS = E // 2
DH_BANKS = 4
G_AHEAD = 4
A_BUFS = 4
GATE_CUTS = (0, 1, 3, E)
VECTOR_W2 = range(2, E, 2)
VECTOR_W1_PAIRS = 2


def tile_moe_bdx_mlp_silu_kernel(tc, dyT, a, w2, w1, gate, offs, pos1, pos2, pos3, out):
    nc = tc.nc
    with ExitStack() as ctx:
        held = ctx.enter_context(tc.tile_pool(name="held", bufs=1))
        ring = ctx.enter_context(tc.tile_pool(name="ring", bufs=1))
        psum = ctx.enter_context(tc.psum_pool(name="psum", bufs=1))

        offs_sb = held.tile([P, S // PER_COLUMN], U16, name="offs_sb")
        pos_sb = [held.tile([P, T // PER_COLUMN], U16, name="pos_sb%d" % r) for r in range(3)]
        dy_rows = dyT.rearrange("(p j) t -> p j t", j=PACK)
        dy_sb = [held.tile([P, T], F32, name="dy_sb%d" % j) for j in range(PACK)]
        gate_sb = {}
        a_rows = a.rearrange("(p t) s -> p t s", t=PACK)
        dh_banks = [psum.tile([P, PACK * SLOT_HALF], F32, name="dh_bank%d" % b) for b in range(DH_BANKS)]
        dx_banks = [dh_banks[2], dh_banks[3], psum.tile([P, 2 * C], F32, name="dx_bank")]
        a_sb = {}
        w2_sb = {}
        w1_sb = {}

        def load_dy(j):
            nc.sync.dma_start(out=dy_sb[j][:], in_=dy_rows[:, j, :])

        def load_gate(piece):
            first, last = GATE_CUTS[piece], GATE_CUTS[piece + 1]
            tile = held.tile([P, (last - first) * C], F32, name="gate_sb%d" % piece)
            nc.sync.dma_start(out=tile[:], in_=gate[0:P, first * C:last * C])
            for e in range(first, last):
                gate_sb[e] = tile[:, (e - first) * C:(e - first + 1) * C]

        def load_a(e):
            a_sb[e] = ring.tile([P, PACK, C], F32, name="a_sb", bufs=A_BUFS)
            nc.sync.dma_start(out=a_sb[e][:], in_=a_rows[:, :, e * C:(e + 1) * C])

        def load_w2(e):
            w2_sb[e] = ring.tile([P, PACK * H], F32, name="w2_sb", tag="w2_or_dx", bufs=E, align_bytes=64)
            nc.sync.dma_start(out=w2_sb[e][:], in_=w2[e].rearrange("(p j) i -> p (j i)", j=PACK))

        def load_w1(e):
            w1_sb[e] = ring.tile([P, PACK, K], F32, name="w1_sb%d" % e, tag="w1_%d" % e, bufs=1)
            nc.sync.dma_start(out=w1_sb[e][:], in_=w1[e].rearrange("(p j) k -> p j k", j=PACK))

        nc.sync.dma_start(offs_sb[:], offs)
        load_dy(0)
        load_gate(0)
        load_gate(1)
        load_dy(1)
        load_a(0)
        load_dy(2)
        load_w2(0)
        load_dy(3)
        load_a(1)
        load_gate(2)
        load_w2(1)
        for e in range(2, A_BUFS):
            load_w2(e)
            load_a(e)
        load_w2(A_BUFS)

        def later_loads(e):
            if e + A_BUFS < E:
                load_a(e + A_BUFS)
            if e + A_BUFS + 1 < E:
                load_w2(e + A_BUFS + 1)
            if e + A_BUFS == E - 1:
                for r, pos in enumerate((pos1, pos2, pos3)):
                    nc.sync.dma_start(pos_sb[r][:], pos)
                for x in range(E):
                    load_w1(x)

        g32 = {}

        def gather_g(e):
            g32[e] = ring.tile([P, PACK, C], F32, name="g32", bufs=G_AHEAD)
            entries = offs_sb[:, e * C // PER_COLUMN:(e + 1) * C // PER_COLUMN]
            for j in range(PACK):
                nc.vector.tensor_tensor(g32[e][:, j, :], dy_sb[j][:].indirect(entries), gate_sb[e], ALU.mult)

        def weave_out(ap):
            return ap.rearrange("p (c i j) -> p c j i", i=RUN, j=PACK)

        def weave_in(ap):
            return ap.rearrange("p j (c i) -> p c j i", i=RUN)

        def quantize(src, width, name, bufs):
            codes = ring.tile([P, width], U32, name=name + "_codes", bufs=bufs, align_bytes=64)
            scales = ring.tile([P, width], U8, name=name + "_scales", bufs=bufs, align_bytes=64)
            nc.vector.quantize_mx(out=codes[:].bitcast(FP8X4), scales=scales[:], in_=src)
            return codes, scales

        def matmul(dst, lhs, lhs_cols, rhs, rhs_cols):
            nc.tensor.matmul_mx(
                out=dst,
                lhsT=lhs[0][:, lhs_cols].bitcast(FP8X4),
                lhsT_scale=lhs[1][:, lhs_cols],
                rhs=rhs[0][:, rhs_cols].bitcast(FP8X4),
                rhs_scale=rhs[1][:, rhs_cols],
                start=True,
                stop=True,
            )

        u = {}
        th = {}
        w2_16 = {}
        da_q = {}

        def make_dh(e):
            g16 = ring.tile([P, PACK * C], BF16, name="g16", bufs=4, align_bytes=64)
            nc.scalar.copy(weave_out(g16[:]), weave_in(g32[e][:]))
            w2_16[e] = ring.tile([P, PACK * H], BF16, name="w2_16", bufs=3, align_bytes=64)
            cast = nc.vector.tensor_copy if e in VECTOR_W2 else nc.scalar.copy
            cast(
                w2_16[e][:].rearrange("p (t m j) -> p m j t", t=PACK, j=PACK),
                w2_sb[e][:].rearrange("p (j m t) -> p m j t", t=PACK, j=PACK),
            )
            u[e] = ring.tile([P, PACK * C], F32, name="u", bufs=3)
            th[e] = ring.tile([P, PACK * C], F32, name="th", bufs=3)
            nc.scalar.activation(weave_out(u[e][:]), weave_in(a_sb[e][:]), ACT.Silu, scale=-1.0)
            nc.scalar.activation(weave_out(th[e][:]), weave_in(a_sb[e][:]), ACT.Tanh, scale=0.5)
            later_loads(e)
            g_q = quantize(g16[:], C, "g", 2)
            w2_q = quantize(w2_16[e][:], H, "w2", 3)
            for h in range(2):
                dh = dh_banks[(2 * e + h) % DH_BANKS]
                for t in range(PACK):
                    matmul(
                        dh[:, t * SLOT_HALF:(t + 1) * SLOT_HALF],
                        w2_q, slice(t * P, (t + 1) * P),
                        g_q, slice(h * SLOT_HALF, (h + 1) * SLOT_HALF),
                    )

        def make_da(e):
            if e + 1 < E:
                partial = w2_16[e + 1][:].bitcast(F32)
            else:
                partial_last = held.tile([P, PACK * C], F32, name="partial_last")
                partial = partial_last[:]
            da16 = ring.tile([P, PACK * C], BF16, name="da16", bufs=3, align_bytes=64)
            for h in range(2):
                cols = slice(h * PACK * SLOT_HALF, (h + 1) * PACK * SLOT_HALF)
                nc.vector.scalar_tensor_tensor(
                    partial[:, cols].rearrange("p (s t) -> p s t", t=PACK),
                    u[e][:, cols].rearrange("p (s t) -> p s t", t=PACK),
                    1.0,
                    dh_banks[(2 * e + h) % DH_BANKS][:].rearrange("p (t s) -> p s t", t=PACK),
                    ALU.subtract,
                    ALU.mult,
                )
            for h in range(2):
                cols = slice(h * PACK * SLOT_HALF, (h + 1) * PACK * SLOT_HALF)
                nc.vector.scalar_tensor_tensor(da16[:, cols], th[e][:, cols], 1.0, partial[:, cols], ALU.add, ALU.mult)
            da_q[e] = quantize(da16[:], C, "da", E)

        for e in range(G_AHEAD):
            gather_g(e)
        for e in range(E):
            make_dh(e)
            if e > 0:
                make_da(e - 1)
            if e + G_AHEAD < E:
                gather_g(e + G_AHEAD)
        make_da(E - 1)

        pair_width = 2 * PACK * P
        w1_q = {}
        for kb in range(K_BLOCKS):
            for pair in range(PAIRS):
                if kb == K_BLOCKS - 1:
                    w1_16 = w2_sb[E - 1][:].bitcast(BF16)[:, pair * pair_width:(pair + 1) * pair_width]
                else:
                    w1_16_tile = ring.tile([P, pair_width], BF16, name="w1_16_tile", bufs=2 * PAIRS, align_bytes=64)
                    w1_16 = w1_16_tile[:]
                for x in range(2):
                    cast = nc.vector.tensor_copy if kb == 0 and pair < VECTOR_W1_PAIRS else nc.scalar.copy
                    cast(
                        weave_out(w1_16[:, x * PACK * P:(x + 1) * PACK * P]),
                        weave_in(w1_sb[2 * pair + x][:, :, kb * P:(kb + 1) * P]),
                    )
                w1_q[kb, pair] = quantize(w1_16, 2 * P, "w1", K_BLOCKS * PAIRS)

        dx = {}
        for kb in range(K_BLOCKS):
            if kb == 0:
                dx[kb] = ring.tile([P, S], F32, name="dx_first", tag="w1_%d" % (E - 1), bufs=1)
            else:
                dx[kb] = ring.tile([P, S], F32, name="dx", tag="w2_or_dx", bufs=E, align_bytes=64)
            for pair in range(PAIRS):
                bank = dx_banks[pair]
                for x in range(2):
                    matmul(
                        bank[:, x * C:(x + 1) * C],
                        w1_q[kb, pair], slice(x * P, (x + 1) * P),
                        da_q[2 * pair + x], slice(0, C),
                    )
                nc.scalar.activation(dx[kb][:, pair * 2 * C:(pair + 1) * 2 * C], bank[:], ACT.Copy, scale=-0.5)

        for kb in range(K_BLOCKS):
            total = {}
            for r in range(3):
                for h in range(2):
                    entries = pos_sb[r][:, h * TOKEN_HALF // PER_COLUMN:(h + 1) * TOKEN_HALF // PER_COLUMN]
                    running = ring.tile([P, TOKEN_HALF], F32, name="running", bufs=8)
                    if r == 0:
                        nc.vector.tensor_copy(running[:], dx[kb][:].indirect(entries))
                    else:
                        nc.vector.tensor_tensor(running[:], dx[kb][:].indirect(entries), total[h][:], ALU.add)
                    total[h] = running
            for h in range(2):
                nc.sync.dma_start(out=out[kb * P:(kb + 1) * P, h * TOKEN_HALF:(h + 1) * TOKEN_HALF], in_=total[h][:])
